import numpy as np
import ml_dtypes


def mxq(x, axis, fmt="e4m3"):
    dtype, down = {"e4m3": (ml_dtypes.float8_e4m3fn, 7), "e5m2": (ml_dtypes.float8_e5m2, 14)}[fmt]
    v = np.moveaxis(np.asarray(x, np.float32).astype(ml_dtypes.bfloat16).astype(np.float64), axis, -1)
    blocks = v.reshape(v.shape[:-1] + (-1, 32))
    amax = np.abs(blocks).max(-1, keepdims=True)
    byte = np.maximum(np.where(amax > 0, np.frexp(amax)[1] - 1 + 127, 0) - down, 1)
    scale = np.exp2(byte - 127.0)
    codes = (blocks / scale).astype(np.float32).astype(dtype).astype(np.float64)
    return np.moveaxis((codes * scale).reshape(v.shape), -1, axis)


WIDE = False


def mx_kscale(k):
    if not WIDE:
        return np.ones(k)
    levels = np.array([24, -24, 12, -12, 0])
    if k % 512:
        return np.exp2(np.random.permutation(np.resize(levels, k // 32))).repeat(32)
    a = np.empty((k // 512, 16))
    for p in range(k // 512):
        a[p, :8] = np.random.permutation(np.resize(levels, 8))
        for g in range(8):
            far = levels[np.abs(levels - a[p, g]) >= 10]
            a[p, g + 8] = far[np.random.randint(len(far))]
    return np.exp2(a.ravel()).repeat(32)


def f64(x):
    return np.asarray(x).astype(np.float64)


def striped(idx):
    return np.tile(idx.reshape(-1, 16).T, (8, 1)).astype(np.uint16)


def unstriped(offs):
    return offs[:16].T.reshape(-1).astype(np.int64)


E2M1 = np.array([0.0, 0.5, 1.0, 1.5, 2.0, 3.0, 4.0, 6.0, -0.0, -0.5, -1.0, -1.5, -2.0, -3.0, -4.0, -6.0])


def pack_weight(w, fmt):
    k, n = w.shape
    w = f64(np.asarray(w, np.float32).astype(ml_dtypes.bfloat16)).reshape(k // 32, 32, n)
    amax = np.abs(w).max(1)
    if fmt == "e4m3":
        byte = np.frexp(amax)[1] - 1 + 127 - 7
    else:
        mant, ex = np.frexp(amax / 6.0)
        byte = np.where(mant > 0.5, ex, ex - 1) + 127
    byte = np.clip(np.where(amax > 0, byte, 1), 1, 254)
    scaled = (w * np.exp2(127.0 - byte)[:, None, :]).reshape(k, n).astype(np.float32)
    by_word = np.ascontiguousarray(scaled.reshape(k // 512, 128, 4, n).transpose(0, 1, 3, 2))
    if fmt == "e4m3":
        words = by_word.astype(ml_dtypes.float8_e4m3fn).view(np.uint8)
    else:
        c = by_word.astype(ml_dtypes.float4_e2m1fn).view(np.uint8) & 0xF
        words = (c[..., 0::2] | (c[..., 1::2] << 4)).reshape(k // 512, 128, 2 * n)
    return np.ascontiguousarray(words), np.ascontiguousarray(byte.astype(np.uint8).reshape(k // 512, 16, n))


def unpack_weight(words, scales, fmt):
    g, _, n = scales.shape
    words = np.ascontiguousarray(words).reshape(g, 128, n, -1)
    if fmt == "e4m3":
        vals = words.view(ml_dtypes.float8_e4m3fn).astype(np.float64)
    else:
        nib = np.empty((g, 128, n, 4), np.uint8)
        nib[..., 0::2] = words & 0xF
        nib[..., 1::2] = words >> 4
        vals = E2M1[nib]
    vals = vals * np.repeat(np.exp2(scales.astype(np.float64) - 127.0), 8, axis=1)[..., None]
    return vals.transpose(0, 1, 3, 2).reshape(g * 512, n)


def pack_table4(v):
    words, scales = pack_weight(v, "e2m1")
    g, t = words.shape[0] // 2, v.shape[1]
    return np.ascontiguousarray(words.reshape(g, 2, 128, t, 2).transpose(0, 2, 3, 1, 4).reshape(g, 128, t, 4)), scales


def unpack_table4(words, scales):
    g, _, t, _ = words.shape
    return unpack_weight(words.reshape(g, 128, t, 2, 2).transpose(0, 3, 1, 2, 4).reshape(2 * g, 128, 2 * t), scales, "e2m1")


def planes(y):
    n, m = y.shape
    v = y.astype(np.float32).astype(ml_dtypes.bfloat16).astype(np.float64).reshape(n // 32, 32, m)
    top = np.abs(v).max(1)
    byte = np.clip(np.where(top > 0, np.frexp(top)[1] - 1 + 127 - 7, 1), 1, 254)
    codes = (v * np.exp2(127.0 - byte)[:, None, :]).reshape(n, m).astype(np.float32).astype(ml_dtypes.float8_e4m3fn).view(np.uint8)
    words = codes.reshape(n // 512, 128, 4, m).transpose(0, 1, 3, 2)
    return np.ascontiguousarray(words), np.ascontiguousarray(byte.astype(np.uint8).reshape(n // 512, 16, m))


def silu(f):
    return f / (1.0 + np.exp(-np.maximum(f, -700.0)))


K, R, N, T, J = 1024, 1024, 512, 2048, 1024


def setup_inputs():
    n = np.random.standard_normal
    s = mx_kscale(K)[:, None]
    u = mx_kscale(R)[:, None]
    p_tab = pack_table4(n((K, T)) * s)
    return {
        "tab_words": p_tab[0],
        "tab_scales": p_tab[1],
        "wu": (n((K, R)) / np.sqrt(K) / s).astype(np.float32),
        "sm": (np.random.uniform(0.5, 2.0, R) * u[:, 0]).astype(np.float32),
        "wd": (n((R, N)) / np.sqrt(R) / u).astype(np.float32),
        "rT": (n((N, T))).astype(np.float32),
        "wgo": np.tile(np.random.uniform(0.5, 2.0, J), (128, 1)).astype(np.float32),
        "offs": striped(np.random.permutation(T)[:J]),
    }


def reference(tab_words, tab_scales, wu, sm, wd, rT, wgo, offs):
    idx = unstriped(offs)
    tab_ = unpack_table4(tab_words, tab_scales)[:, idx]
    wu_ = mxq(f64(wu), 0, "e4m3")
    a = wu_.T @ tab_
    h = f64(sm)[:, None] * silu(a)
    h_ = mxq(h, 0, "e4m3")
    wd_ = mxq(f64(wd), 0, "e4m3")
    y = wd_.T @ h_
    out = np.zeros((N, T))
    out[:, idx] = f64(wgo)[0] * (y + f64(rT)[:, idx])
    return (out,) + planes(out)

@@ -1,0 +1,206 @@
+from contextlib import ExitStack
+
+import concourse.mybir as mybir
+
+K, R, N, T, J = 1024, 1024, 512, 2048, 1024
+FLOPS = 2 * K * R * J + 2 * R * N * J
+
+F32 = mybir.dt.float32
+BF16 = mybir.dt.bfloat16
+I32 = mybir.dt.int32
+U32 = mybir.dt.uint32
+U16 = mybir.dt.uint16
+U8 = mybir.dt.uint8
+FP8X4 = mybir.dt.float8_e4m3fn_x4
+FP4X4 = mybir.dt.float4_e2m1fn_x4
+ACT = mybir.ActivationFunctionType
+ALU = mybir.AluOpType
+
+P = 128
+PACK = 4
+KP = P * PACK
+CH = 128
+GRP = 256
+OC = 512
+
+
+def tile_list_modp_silu_resP_kernel(
+    tc, tab_words, tab_scales, wu, sm, wd, rT, wgo, offs, out_0, out_1, out_2
+):
+    nc = tc.nc
+    with ExitStack() as ctx:
+        keep = ctx.enter_context(tc.tile_pool(name="keep", bufs=1))
+        big = ctx.enter_context(tc.tile_pool(name="big", bufs=4))
+        work = ctx.enter_context(tc.tile_pool(name="work", bufs=3))
+        ps1 = ctx.enter_context(tc.psum_pool(name="ps1", bufs=4))
+        ps2 = ctx.enter_context(tc.psum_pool(name="ps2", bufs=4))
+
+        offsets = keep.tile([P, J // 16], U16, name="offsets")
+        nc.sync.dma_start(offsets[:], offs)
+
+        tabw = big.tile([P, T], I32, name="tabw", tag="big", align_bytes=64)
+        nc.sync.dma_start(tabw[:], tab_words[0].rearrange("p t b -> p (t b)").bitcast(I32))
+
+        tabs = keep.tile([P, T], U8, name="tabs", align_bytes=64)
+        nc.vector.memset(tabs[:].bitcast(I32), 0)
+        gs1 = keep.tile([P, J], U8, name="gs1", align_bytes=64)
+        nc.vector.memset(gs1[:].bitcast(I32), 0)
+        for q in range(4):
+            nc.scalar.dma_start(
+                tabs[32 * q : 32 * q + 8, :].bitcast(I32),
+                tab_scales[:, 4 * q : 4 * q + 4, :].bitcast(I32),
+            )
+
+        pages = []
+        for i in range(PACK):
+            page = keep.tile([P, T], F32, name="page%d" % i, tag="page%d" % i, align_bytes=64)
+            nc.vector.memset(page[:], 0.0)
+            pages.append(page)
+
+        gs0 = keep.tile([P, J], U8, name="gs0", align_bytes=64)
+        nc.vector.tensor_copy(gs0[:], tabs[:].indirect(offsets[:]))
+        for q in range(4):
+            nc.gpsimd.dma_start(
+                gs1[32 * q : 32 * q + 4, :].bitcast(I32), gs0[32 * q + 4 : 32 * q + 8, :].bitcast(I32)
+            )
+        gw = keep.tile([P, J], U32, name="gw", align_bytes=64)
+        nc.vector.tensor_copy(gw[:], tabw[:].bitcast(U32).indirect(offsets[:]))
+        parted = keep.tile([P, 2 * J], U16, name="parted", align_bytes=64)
+        nc.vector.tensor_copy(
+            parted[:].rearrange("p (d j) -> p d j", d=2),
+            gw[:].bitcast(U16).rearrange("p (j d) -> p d j", d=2),
+        )
+        gsc = [gs0, gs1]
+
+        def weight_block(rows, name, on_vector):
+            raw = big.tile([P, T], F32, name="raw_" + name, tag="big", align_bytes=64)
+            nc.sync.dma_start(
+                raw[:].rearrange("p (j c) -> p j c", j=PACK), rows.rearrange("(p j) c -> p j c", j=PACK)
+            )
+            grouped = work.tile([P, PACK * KP], BF16, name="grp_" + name, tag="grouped", align_bytes=64)
+            dst = grouped[:].rearrange("p (t m j) -> p m j t", t=PACK, j=PACK)
+            srcv = raw[:].rearrange("p (j m t) -> p m j t", j=PACK, t=PACK)
+            if on_vector:
+                nc.vector.tensor_copy(dst, srcv)
+            else:
+                for u in range(2):
+                    nc.scalar.copy(dst[:, 64 * u : 64 * (u + 1)], srcv[:, 64 * u : 64 * (u + 1)])
+            codes = keep.tile([P, KP], U32, name="codes_" + name, align_bytes=64)
+            scales = keep.tile([P, KP], U8, name="scales_" + name, align_bytes=64)
+            nc.vector.quantize_mx(codes[:].bitcast(FP8X4), scales[:], grouped[:])
+            return codes, scales
+
+        wuq = {}
+        for b in range(2):
+            for a in range(2):
+                wuq[b, a] = weight_block(
+                    wu[KP * a : KP * (a + 1), KP * b : KP * (b + 1)], "wu%d%d" % (b, a), a == 1
+                )
+            if b == 0:
+                smt = keep.tile([P, 2, PACK], F32, name="smt")
+                nc.gpsimd.dma_start(smt[:], sm.rearrange("(b p t) -> p b t", b=2, t=PACK))
+        wdq = [weight_block(wd[KP * b : KP * (b + 1), :], "wd%d" % b, b == 1) for b in range(2)]
+
+        wg = big.tile([P, J], F32, name="wg", tag="big", align_bytes=64)
+        nc.sync.dma_start(wg[:], wgo)
+        rts = []
+        for i in range(PACK):
+            rt = big.tile([P, T], F32, name="rt%d" % i, tag="big", align_bytes=64)
+            nc.sync.dma_start(rt[:], rT.rearrange("(p i) t -> p i t", i=PACK)[:, i, :])
+            rts.append(rt)
+
+        hq = {}
+        for b in range(2):
+            for half in range(2):
+                hq[b, half] = (
+                    keep.tile([P, KP], U32, name="hc%d%d" % (b, half), align_bytes=64),
+                    keep.tile([P, KP], U8, name="hs%d%d" % (b, half), align_bytes=64),
+                )
+
+        def hidden(b, c):
+            j0 = c * CH
+            bank = ps1.tile([P, PACK, CH], F32, name="a_bank", tag="a")
+            for t in range(PACK):
+                for a in range(2):
+                    codes, scales = wuq[b, a]
+                    nc.tensor.matmul_mx(
+                        bank[:, t, :],
+                        lhsT=codes[:, P * t : P * (t + 1)].bitcast(FP8X4),
+                        lhsT_scale=scales[:, P * t : P * (t + 1)],
+                        rhs=parted[:, a * J + j0 : a * J + j0 + CH].bitcast(FP4X4),
+                        rhs_scale=gsc[a][:, j0 : j0 + CH],
+                        start=(a == 0),
+                        stop=(a == 1),
+                    )
+            act = work.tile([P, CH, PACK], F32, name="act", tag="act", bufs=4, align_bytes=64)
+            nc.scalar.activation(act[:], bank[:].rearrange("p t j -> p j t"), ACT.Silu)
+            hb = work.tile([P, CH, PACK], BF16, name="hb", tag="hb", bufs=4, align_bytes=64)
+            nc.vector.tensor_tensor(hb[:], act[:], smt[:, b : b + 1, :].to_broadcast([P, CH, PACK]), ALU.mult)
+            codes, scales = hq[b, j0 // KP]
+            o = j0 % KP
+            nc.vector.quantize_mx(
+                codes[:, o : o + CH].bitcast(FP8X4), scales[:, o : o + CH], hb[:].rearrange("p j t -> p (j t)")
+            )
+
+        def place(i, j0, width, last=False):
+            half, o = j0 // KP, j0 % KP
+            bank = ps2.tile([P, KP], F32, name="y_bank", tag="y")
+            for b in range(2):
+                nc.tensor.matmul_mx(
+                    bank[:, :width],
+                    lhsT=wdq[b][0][:, P * i : P * (i + 1)].bitcast(FP8X4),
+                    lhsT_scale=wdq[b][1][:, P * i : P * (i + 1)],
+                    rhs=hq[b, half][0][:, o : o + width].bitcast(FP8X4),
+                    rhs_scale=hq[b, half][1][:, o : o + width],
+                    start=(b == 0),
+                    stop=(b == 1),
+                )
+            if last:
+                y = keep.tile([P, KP], F32, name="y_last", tag="page2", align_bytes=64)
+            else:
+                y = work.tile([P, KP], F32, name="y", tag="y", bufs=4, align_bytes=64)
+            nc.scalar.copy(y[:, :width], bank[:, :width])
+            sl = offsets[:, j0 // 16 : (j0 + width) // 16]
+            z = work.tile([P, KP], F32, name="z", tag="z", align_bytes=64)
+            nc.vector.tensor_tensor(z[:, :width], rts[i][:].indirect(sl), y[:, :width], ALU.add)
+            nc.vector.tensor_tensor(pages[i][:].indirect(sl), z[:, :width], wg[:, j0 : j0 + width], ALU.mult)
+
+        woven = [keep.tile([P, OC, PACK], BF16, name="woven%d" % c, align_bytes=64) for c in range(T // OC)]
+        ocodes = [keep.tile([P, OC], U32, name="ocodes%d" % c, align_bytes=64) for c in range(T // OC)]
+        oscales = keep.tile([P, T], U8, name="oscales", align_bytes=64)
+        out_rows = out_0.rearrange("(p i) t -> p i t", i=PACK)
+        out_words = out_1[0].rearrange("p t b -> p (t b)").bitcast(I32)
+
+        def finish(i):
+            nc.sync.dma_start(out_rows[:, i, :], pages[i][:])
+            for c in (2, 3, 0, 1):
+                if i == PACK - 1 and c >= 2:
+                    nc.vector.tensor_copy(woven[c][:, :, i], pages[i][:, c * OC : (c + 1) * OC])
+                else:
+                    nc.scalar.copy(woven[c][:, :, i], pages[i][:, c * OC : (c + 1) * OC])
+                if i == PACK - 1:
+                    nc.vector.quantize_mx(
+                        ocodes[c][:].bitcast(FP8X4),
+                        oscales[:, c * OC : (c + 1) * OC],
+                        woven[c][:].rearrange("p j t -> p (j t)"),
+                    )
+                    nc.sync.dma_start(out_words[:, c * OC : (c + 1) * OC], ocodes[c][:].bitcast(I32))
+
+        for g in range(J // GRP):
+            for b in range(2):
+                for c in range(g * GRP // CH, (g + 1) * GRP // CH):
+                    hidden(b, c)
+            place(0, g * GRP, GRP)
+        for i in range(1, PACK - 1):
+            for half in range(2):
+                place(i, half * KP, KP)
+            finish(i - 1)
+        place(3, 0, KP)
+        place(3, KP, GRP)
+        finish(2)
+        place(3, KP + GRP, GRP, last=True)
+        finish(3)
+        for q in range(4):
+            nc.scalar.dma_start(
+                out_2[0, 4 * q : 4 * q + 4, :].bitcast(I32), oscales[32 * q : 32 * q + 4, :].bitcast(I32)
+            )

@@ -22,6 +22,8 @@ KP = P * PACK
 CH = 128
 GRP = 256
 OC = 512
+ON_SCALAR = ((1, 1), (1, 2), (1, 3))
+WEAVE = {"wu00": "SS", "wu01": "SS", "wu10": "SS", "wu11": "VV", "wd0": "SS", "wd1": "VV"}
 
 
 def tile_list_modp_silu_resP_kernel(
@@ -38,41 +40,26 @@ def tile_list_modp_silu_resP_kernel(
         offsets = keep.tile([P, J // 16], U16, name="offsets")
         nc.sync.dma_start(offsets[:], offs)
 
-        tabw = big.tile([P, T], I32, name="tabw", tag="big", align_bytes=64)
-        nc.sync.dma_start(tabw[:], tab_words[0].rearrange("p t b -> p (t b)").bitcast(I32))
-
+        smt = keep.tile([P, 2, PACK], F32, name="smt")
+        nc.sync.dma_start(smt[:], sm.rearrange("(b p t) -> p b t", b=2, t=PACK))
         tabs = keep.tile([P, T], U8, name="tabs", align_bytes=64)
-        nc.vector.memset(tabs[:].bitcast(I32), 0)
+        nc.gpsimd.memset(tabs[:].bitcast(I32), 0)
         gs1 = keep.tile([P, J], U8, name="gs1", align_bytes=64)
-        nc.vector.memset(gs1[:].bitcast(I32), 0)
+        nc.gpsimd.memset(gs1[:].bitcast(I32), 0)
         for q in range(4):
-            nc.scalar.dma_start(
+            nc.sync.dma_start(
                 tabs[32 * q : 32 * q + 8, :].bitcast(I32),
                 tab_scales[:, 4 * q : 4 * q + 4, :].bitcast(I32),
             )
-
-        pages = []
-        for i in range(PACK):
-            page = keep.tile([P, T], F32, name="page%d" % i, tag="page%d" % i, align_bytes=64)
-            nc.vector.memset(page[:], 0.0)
-            pages.append(page)
-
         gs0 = keep.tile([P, J], U8, name="gs0", align_bytes=64)
         nc.vector.tensor_copy(gs0[:], tabs[:].indirect(offsets[:]))
         for q in range(4):
-            nc.gpsimd.dma_start(
+            nc.scalar.dma_start(
                 gs1[32 * q : 32 * q + 4, :].bitcast(I32), gs0[32 * q + 4 : 32 * q + 8, :].bitcast(I32)
             )
-        gw = keep.tile([P, J], U32, name="gw", align_bytes=64)
-        nc.vector.tensor_copy(gw[:], tabw[:].bitcast(U32).indirect(offsets[:]))
-        parted = keep.tile([P, 2 * J], U16, name="parted", align_bytes=64)
-        nc.vector.tensor_copy(
-            parted[:].rearrange("p (d j) -> p d j", d=2),
-            gw[:].bitcast(U16).rearrange("p (j d) -> p d j", d=2),
-        )
         gsc = [gs0, gs1]
 
-        def weight_block(rows, name, on_vector):
+        def weight_block(rows, name, engines):
             raw = big.tile([P, T], F32, name="raw_" + name, tag="big", align_bytes=64)
             nc.sync.dma_start(
                 raw[:].rearrange("p (j c) -> p j c", j=PACK), rows.rearrange("(p j) c -> p j c", j=PACK)
@@ -80,34 +67,50 @@ def tile_list_modp_silu_resP_kernel(
             grouped = work.tile([P, PACK * KP], BF16, name="grp_" + name, tag="grouped", align_bytes=64)
             dst = grouped[:].rearrange("p (t m j) -> p m j t", t=PACK, j=PACK)
             srcv = raw[:].rearrange("p (j m t) -> p m j t", j=PACK, t=PACK)
-            if on_vector:
+            if engines == "VV":
                 nc.vector.tensor_copy(dst, srcv)
             else:
                 for u in range(2):
-                    nc.scalar.copy(dst[:, 64 * u : 64 * (u + 1)], srcv[:, 64 * u : 64 * (u + 1)])
+                    copy = nc.vector.tensor_copy if engines[u] == "V" else nc.scalar.copy
+                    copy(dst[:, 64 * u : 64 * (u + 1)], srcv[:, 64 * u : 64 * (u + 1)])
             codes = keep.tile([P, KP], U32, name="codes_" + name, align_bytes=64)
             scales = keep.tile([P, KP], U8, name="scales_" + name, align_bytes=64)
             nc.vector.quantize_mx(codes[:].bitcast(FP8X4), scales[:], grouped[:])
             return codes, scales
 
-        wuq = {}
-        for b in range(2):
-            for a in range(2):
-                wuq[b, a] = weight_block(
-                    wu[KP * a : KP * (a + 1), KP * b : KP * (b + 1)], "wu%d%d" % (b, a), a == 1
-                )
-            if b == 0:
-                smt = keep.tile([P, 2, PACK], F32, name="smt")
-                nc.gpsimd.dma_start(smt[:], sm.rearrange("(b p t) -> p b t", b=2, t=PACK))
-        wdq = [weight_block(wd[KP * b : KP * (b + 1), :], "wd%d" % b, b == 1) for b in range(2)]
+        def wu_block(b, a):
+            name = "wu%d%d" % (b, a)
+            return weight_block(wu[KP * a : KP * (a + 1), KP * b : KP * (b + 1)], name, WEAVE[name])
+
+        wuq = {(0, 0): wu_block(0, 0)}
+        tabw = big.tile([P, T], I32, name="tabw", tag="big", align_bytes=64)
+        nc.sync.dma_start(tabw[:], tab_words[0].rearrange("p t b -> p (t b)").bitcast(I32))
+        gw = keep.tile([P, J], U32, name="gw", align_bytes=64)
+        nc.vector.tensor_copy(gw[:], tabw[:].bitcast(U32).indirect(offsets[:]))
+        parted = keep.tile([P, 2 * J], U16, name="parted", align_bytes=64)
+        nc.vector.tensor_copy(
+            parted[:].rearrange("p (d j) -> p d j", d=2),
+            gw[:].bitcast(U16).rearrange("p (j d) -> p d j", d=2),
+        )
+        for b, a in ((0, 1), (1, 0), (1, 1)):
+            wuq[b, a] = wu_block(b, a)
+        wdq = [weight_block(wd[KP * b : KP * (b + 1), :], "wd%d" % b, WEAVE["wd%d" % b]) for b in range(2)]
+
+        pages = []
+        for i in range(PACK):
+            page = keep.tile([P, T], F32, name="page%d" % i, tag="page%d" % i, align_bytes=64)
+            nc.vector.memset(page[:], 0.0)
+            pages.append(page)
 
         wg = big.tile([P, J], F32, name="wg", tag="big", align_bytes=64)
-        nc.sync.dma_start(wg[:], wgo)
+        nc.sync.dma_start(wg[:, :GRP], wgo[:, :GRP])
         rts = []
         for i in range(PACK):
             rt = big.tile([P, T], F32, name="rt%d" % i, tag="big", align_bytes=64)
             nc.sync.dma_start(rt[:], rT.rearrange("(p i) t -> p i t", i=PACK)[:, i, :])
             rts.append(rt)
+            if i == 0:
+                nc.sync.dma_start(wg[:, GRP:], wgo[:, GRP:])
 
         hq = {}
         for b in range(2):
@@ -117,30 +120,58 @@ def tile_list_modp_silu_resP_kernel(
                     keep.tile([P, KP], U8, name="hs%d%d" % (b, half), align_bytes=64),
                 )
 
-        def hidden(b, c):
-            j0 = c * CH
-            bank = ps1.tile([P, PACK, CH], F32, name="a_bank", tag="a")
-            for t in range(PACK):
-                for a in range(2):
-                    codes, scales = wuq[b, a]
-                    nc.tensor.matmul_mx(
-                        bank[:, t, :],
-                        lhsT=codes[:, P * t : P * (t + 1)].bitcast(FP8X4),
-                        lhsT_scale=scales[:, P * t : P * (t + 1)],
-                        rhs=parted[:, a * J + j0 : a * J + j0 + CH].bitcast(FP4X4),
-                        rhs_scale=gsc[a][:, j0 : j0 + CH],
-                        start=(a == 0),
-                        stop=(a == 1),
+        def up(out, b, t, j0, width):
+            for a in range(2):
+                codes, scales = wuq[b, a]
+                nc.tensor.matmul_mx(
+                    out,
+                    lhsT=codes[:, P * t : P * (t + 1)].bitcast(FP8X4),
+                    lhsT_scale=scales[:, P * t : P * (t + 1)],
+                    rhs=parted[:, a * J + j0 : a * J + j0 + width].bitcast(FP4X4),
+                    rhs_scale=gsc[a][:, j0 : j0 + width],
+                    start=(a == 0),
+                    stop=(a == 1),
+                )
+
+        def hidden(b, g):
+            j0 = g * GRP
+            act = work.tile([P, PACK * GRP], F32, name="act", tag="act", align_bytes=64)
+            hb = work.tile([P, PACK * GRP], BF16, name="hb", tag="hb", align_bytes=64)
+            if (b, g) in ON_SCALAR:
+                pairs = work.tile([P, 2, GRP, 2], BF16, name="pairs", tag="pairs", bufs=2, align_bytes=64)
+                for u in range(2):
+                    bank = ps1.tile([P, 2 * GRP], F32, name="a_bank", tag="a")
+                    for e in range(2):
+                        up(bank[:, e * GRP : (e + 1) * GRP], b, 2 * u + e, j0, GRP)
+                    nc.scalar.activation(act[:, 2 * u * GRP : 2 * (u + 1) * GRP], bank[:], ACT.Silu)
+                    for e in range(2):
+                        t = 2 * u + e
+                        nc.scalar.activation(
+                            pairs[:, u, :, e], act[:, t * GRP : (t + 1) * GRP], ACT.Copy, scale=smt[:, b, t : t + 1]
+                        )
+                nc.vector.tensor_copy(
+                    hb[:].bitcast(F32).rearrange("p (j u) -> p j u", u=2),
+                    pairs[:].rearrange("p u j e -> p (u j e)").bitcast(F32).rearrange("p (u j) -> p j u", u=2),
+                )
+            else:
+                for c in range(GRP // CH):
+                    bank = ps1.tile([P, PACK * CH], F32, name="a_bank", tag="a")
+                    for t in range(PACK):
+                        up(bank[:, t * CH : (t + 1) * CH], b, t, j0 + c * CH, CH)
+                    nc.scalar.activation(
+                        act[:, c * KP : (c + 1) * KP].rearrange("p (j t) -> p j t", t=PACK),
+                        bank[:].rearrange("p (t j) -> p j t", t=PACK),
+                        ACT.Silu,
                     )
-            act = work.tile([P, CH, PACK], F32, name="act", tag="act", bufs=4, align_bytes=64)
-            nc.scalar.activation(act[:], bank[:].rearrange("p t j -> p j t"), ACT.Silu)
-            hb = work.tile([P, CH, PACK], BF16, name="hb", tag="hb", bufs=4, align_bytes=64)
-            nc.vector.tensor_tensor(hb[:], act[:], smt[:, b : b + 1, :].to_broadcast([P, CH, PACK]), ALU.mult)
+                nc.vector.tensor_tensor(
+                    hb[:].rearrange("p (j t) -> p j t", t=PACK),
+                    act[:].rearrange("p (j t) -> p j t", t=PACK),
+                    smt[:, b : b + 1, :].to_broadcast([P, GRP, PACK]),
+                    ALU.mult,
+                )
             codes, scales = hq[b, j0 // KP]
             o = j0 % KP
-            nc.vector.quantize_mx(
-                codes[:, o : o + CH].bitcast(FP8X4), scales[:, o : o + CH], hb[:].rearrange("p j t -> p (j t)")
-            )
+            nc.vector.quantize_mx(codes[:, o : o + GRP].bitcast(FP8X4), scales[:, o : o + GRP], hb[:])
 
         def place(i, j0, width, last=False):
             half, o = j0 // KP, j0 % KP
@@ -188,8 +219,7 @@ def tile_list_modp_silu_resP_kernel(
 
         for g in range(J // GRP):
             for b in range(2):
-                for c in range(g * GRP // CH, (g + 1) * GRP // CH):
-                    hidden(b, c)
+                hidden(b, g)
             place(0, g * GRP, GRP)
         for i in range(1, PACK - 1):
             for half in range(2):

@@ -23,6 +23,7 @@ CH = 128
 GRP = 256
 OC = 512
 ON_SCALAR = ((1, 1), (1, 2), (1, 3))
+GROUPED = {"wu00": "ga", "wu01": "gb", "wu10": "ga", "wu11": "gv", "wd0": "ga", "wd1": "gv"}
 WEAVE = {"wu00": "SS", "wu01": "SS", "wu10": "SS", "wu11": "VV", "wd0": "SS", "wd1": "VV"}
 
 
@@ -54,7 +55,7 @@ def tile_list_modp_silu_resP_kernel(
         gs0 = keep.tile([P, J], U8, name="gs0", align_bytes=64)
         nc.vector.tensor_copy(gs0[:], tabs[:].indirect(offsets[:]))
         for q in range(4):
-            nc.scalar.dma_start(
+            nc.sync.dma_start(
                 gs1[32 * q : 32 * q + 4, :].bitcast(I32), gs0[32 * q + 4 : 32 * q + 8, :].bitcast(I32)
             )
         gsc = [gs0, gs1]
@@ -64,7 +65,7 @@ def tile_list_modp_silu_resP_kernel(
             nc.sync.dma_start(
                 raw[:].rearrange("p (j c) -> p j c", j=PACK), rows.rearrange("(p j) c -> p j c", j=PACK)
             )
-            grouped = work.tile([P, PACK * KP], BF16, name="grp_" + name, tag="grouped", align_bytes=64)
+            grouped = keep.tile([P, PACK * KP], BF16, name="grp_" + name, tag=GROUPED[name], align_bytes=64)
             dst = grouped[:].rearrange("p (t m j) -> p m j t", t=PACK, j=PACK)
             srcv = raw[:].rearrange("p (j m t) -> p m j t", j=PACK, t=PACK)
             if engines == "VV":
@@ -73,7 +74,8 @@ def tile_list_modp_silu_resP_kernel(
                 for u in range(2):
                     copy = nc.vector.tensor_copy if engines[u] == "V" else nc.scalar.copy
                     copy(dst[:, 64 * u : 64 * (u + 1)], srcv[:, 64 * u : 64 * (u + 1)])
-            codes = keep.tile([P, KP], U32, name="codes_" + name, align_bytes=64)
+            tag = "gw" if name == "wu01" else "codes_" + name
+            codes = keep.tile([P, KP], U32, name="codes_" + name, tag=tag, align_bytes=64)
             scales = keep.tile([P, KP], U8, name="scales_" + name, align_bytes=64)
             nc.vector.quantize_mx(codes[:].bitcast(FP8X4), scales[:], grouped[:])
             return codes, scales
@@ -85,7 +87,7 @@ def tile_list_modp_silu_resP_kernel(
         wuq = {(0, 0): wu_block(0, 0)}
         tabw = big.tile([P, T], I32, name="tabw", tag="big", align_bytes=64)
         nc.sync.dma_start(tabw[:], tab_words[0].rearrange("p t b -> p (t b)").bitcast(I32))
-        gw = keep.tile([P, J], U32, name="gw", align_bytes=64)
+        gw = keep.tile([P, J], U32, name="gw", tag="gw", align_bytes=64)
         nc.vector.tensor_copy(gw[:], tabw[:].bitcast(U32).indirect(offsets[:]))
         parted = keep.tile([P, 2 * J], U16, name="parted", align_bytes=64)
         nc.vector.tensor_copy(
@@ -94,23 +96,6 @@ def tile_list_modp_silu_resP_kernel(
         )
         for b, a in ((0, 1), (1, 0), (1, 1)):
             wuq[b, a] = wu_block(b, a)
-        wdq = [weight_block(wd[KP * b : KP * (b + 1), :], "wd%d" % b, WEAVE["wd%d" % b]) for b in range(2)]
-
-        pages = []
-        for i in range(PACK):
-            page = keep.tile([P, T], F32, name="page%d" % i, tag="page%d" % i, align_bytes=64)
-            nc.vector.memset(page[:], 0.0)
-            pages.append(page)
-
-        wg = big.tile([P, J], F32, name="wg", tag="big", align_bytes=64)
-        nc.sync.dma_start(wg[:, :GRP], wgo[:, :GRP])
-        rts = []
-        for i in range(PACK):
-            rt = big.tile([P, T], F32, name="rt%d" % i, tag="big", align_bytes=64)
-            nc.sync.dma_start(rt[:], rT.rearrange("(p i) t -> p i t", i=PACK)[:, i, :])
-            rts.append(rt)
-            if i == 0:
-                nc.sync.dma_start(wg[:, GRP:], wgo[:, GRP:])
 
         hq = {}
         for b in range(2):
@@ -173,6 +158,26 @@ def tile_list_modp_silu_resP_kernel(
             o = j0 % KP
             nc.vector.quantize_mx(codes[:, o : o + GRP].bitcast(FP8X4), scales[:, o : o + GRP], hb[:])
 
+        for b in range(2):
+            hidden(b, 0)
+        wdq = [weight_block(wd[KP * b : KP * (b + 1), :], "wd%d" % b, WEAVE["wd%d" % b]) for b in range(2)]
+
+        pages = []
+        for i in range(PACK):
+            page = keep.tile([P, T], F32, name="page%d" % i, tag="page%d" % i, align_bytes=64)
+            nc.vector.memset(page[:], 0.0)
+            pages.append(page)
+
+        wg = big.tile([P, J], F32, name="wg", tag="big", align_bytes=64)
+        nc.sync.dma_start(wg[:, :GRP], wgo[:, :GRP])
+        rts = []
+        for i in range(PACK):
+            rt = big.tile([P, T], F32, name="rt%d" % i, tag="big", align_bytes=64)
+            nc.sync.dma_start(rt[:], rT.rearrange("(p i) t -> p i t", i=PACK)[:, i, :])
+            rts.append(rt)
+            if i == 0:
+                nc.sync.dma_start(wg[:, GRP:], wgo[:, GRP:])
+
         def place(i, j0, width, last=False):
             half, o = j0 // KP, j0 % KP
             bank = ps2.tile([P, KP], F32, name="y_bank", tag="y")
@@ -218,9 +223,10 @@ def tile_list_modp_silu_resP_kernel(
                     nc.sync.dma_start(out_words[:, c * OC : (c + 1) * OC], ocodes[c][:].bitcast(I32))
 
         for g in range(J // GRP):
-            for b in range(2):
-                hidden(b, g)
             place(0, g * GRP, GRP)
+            if g + 1 < J // GRP:
+                for b in range(2):
+                    hidden(b, g + 1)
         for i in range(1, PACK - 1):
             for half in range(2):
                 place(i, half * KP, KP)

@@ -43,22 +43,15 @@ def tile_list_modp_silu_resP_kernel(
 
         smt = keep.tile([P, 2, PACK], F32, name="smt")
         nc.sync.dma_start(smt[:], sm.rearrange("(b p t) -> p b t", b=2, t=PACK))
-        tabs = keep.tile([P, T], U8, name="tabs", align_bytes=64)
+        tabs = keep.tile([P, T], U8, name="tabs", tag="tabs", align_bytes=64)
         nc.gpsimd.memset(tabs[:].bitcast(I32), 0)
         gs1 = keep.tile([P, J], U8, name="gs1", align_bytes=64)
         nc.gpsimd.memset(gs1[:].bitcast(I32), 0)
         for q in range(4):
-            nc.sync.dma_start(
+            nc.scalar.dma_start(
                 tabs[32 * q : 32 * q + 8, :].bitcast(I32),
                 tab_scales[:, 4 * q : 4 * q + 4, :].bitcast(I32),
             )
-        gs0 = keep.tile([P, J], U8, name="gs0", align_bytes=64)
-        nc.vector.tensor_copy(gs0[:], tabs[:].indirect(offsets[:]))
-        for q in range(4):
-            nc.sync.dma_start(
-                gs1[32 * q : 32 * q + 4, :].bitcast(I32), gs0[32 * q + 4 : 32 * q + 8, :].bitcast(I32)
-            )
-        gsc = [gs0, gs1]
 
         def weight_block(rows, name, engines):
             raw = big.tile([P, T], F32, name="raw_" + name, tag="big", align_bytes=64)
@@ -74,7 +67,7 @@ def tile_list_modp_silu_resP_kernel(
                 for u in range(2):
                     copy = nc.vector.tensor_copy if engines[u] == "V" else nc.scalar.copy
                     copy(dst[:, 64 * u : 64 * (u + 1)], srcv[:, 64 * u : 64 * (u + 1)])
-            tag = "gw" if name == "wu01" else "codes_" + name
+            tag = "tabs" if name == "wu00" else "codes_" + name
             codes = keep.tile([P, KP], U32, name="codes_" + name, tag=tag, align_bytes=64)
             scales = keep.tile([P, KP], U8, name="scales_" + name, align_bytes=64)
             nc.vector.quantize_mx(codes[:].bitcast(FP8X4), scales[:], grouped[:])
@@ -84,7 +77,6 @@ def tile_list_modp_silu_resP_kernel(
             name = "wu%d%d" % (b, a)
             return weight_block(wu[KP * a : KP * (a + 1), KP * b : KP * (b + 1)], name, WEAVE[name])
 
-        wuq = {(0, 0): wu_block(0, 0)}
         tabw = big.tile([P, T], I32, name="tabw", tag="big", align_bytes=64)
         nc.sync.dma_start(tabw[:], tab_words[0].rearrange("p t b -> p (t b)").bitcast(I32))
         gw = keep.tile([P, J], U32, name="gw", tag="gw", align_bytes=64)
@@ -94,8 +86,14 @@ def tile_list_modp_silu_resP_kernel(
             parted[:].rearrange("p (d j) -> p d j", d=2),
             gw[:].bitcast(U16).rearrange("p (j d) -> p d j", d=2),
         )
-        for b, a in ((0, 1), (1, 0), (1, 1)):
-            wuq[b, a] = wu_block(b, a)
+        gs0 = keep.tile([P, J], U8, name="gs0", tag="gw", align_bytes=64)
+        nc.vector.tensor_copy(gs0[:], tabs[:].indirect(offsets[:]))
+        for q in range(4):
+            nc.sync.dma_start(
+                gs1[32 * q : 32 * q + 4, :].bitcast(I32), gs0[32 * q + 4 : 32 * q + 8, :].bitcast(I32)
+            )
+        gsc = [gs0, gs1]
+        wuq = {(b, a): wu_block(b, a) for b in range(2) for a in range(2)}
 
         hq = {}
         for b in range(2):

@@ -48,14 +48,15 @@ def tile_list_modp_silu_resP_kernel(
         gs1 = keep.tile([P, J], U8, name="gs1", align_bytes=64)
         nc.gpsimd.memset(gs1[:].bitcast(I32), 0)
         for q in range(4):
-            nc.scalar.dma_start(
+            nc.sync.dma_start(
                 tabs[32 * q : 32 * q + 8, :].bitcast(I32),
                 tab_scales[:, 4 * q : 4 * q + 4, :].bitcast(I32),
             )
 
         def weight_block(rows, name, engines):
             raw = big.tile([P, T], F32, name="raw_" + name, tag="big", align_bytes=64)
-            nc.sync.dma_start(
+            queue = nc.scalar if name == "wu00" else nc.sync
+            queue.dma_start(
                 raw[:].rearrange("p (j c) -> p j c", j=PACK), rows.rearrange("(p j) c -> p j c", j=PACK)
             )
             grouped = keep.tile([P, PACK * KP], BF16, name="grp_" + name, tag=GROUPED[name], align_bytes=64)
@@ -78,7 +79,7 @@ def tile_list_modp_silu_resP_kernel(
             return weight_block(wu[KP * a : KP * (a + 1), KP * b : KP * (b + 1)], name, WEAVE[name])
 
         tabw = big.tile([P, T], I32, name="tabw", tag="big", align_bytes=64)
-        nc.sync.dma_start(tabw[:], tab_words[0].rearrange("p t b -> p (t b)").bitcast(I32))
+        nc.scalar.dma_start(tabw[:], tab_words[0].rearrange("p t b -> p (t b)").bitcast(I32))
         gw = keep.tile([P, J], U32, name="gw", tag="gw", align_bytes=64)
         nc.vector.tensor_copy(gw[:], tabw[:].bitcast(U32).indirect(offsets[:]))
         parted = keep.tile([P, 2 * J], U16, name="parted", align_bytes=64)

from contextlib import ExitStack

import concourse.mybir as mybir

K, R, N, T, J = 1024, 1024, 512, 2048, 1024
FLOPS = 2 * K * R * J + 2 * R * N * J

F32 = mybir.dt.float32
BF16 = mybir.dt.bfloat16
I32 = mybir.dt.int32
U32 = mybir.dt.uint32
U16 = mybir.dt.uint16
U8 = mybir.dt.uint8
FP8X4 = mybir.dt.float8_e4m3fn_x4
FP4X4 = mybir.dt.float4_e2m1fn_x4
ACT = mybir.ActivationFunctionType
ALU = mybir.AluOpType

P = 128
PACK = 4
KP = P * PACK
CH = 128
GRP = 256
OC = 512
ON_SCALAR = ((1, 1), (1, 2), (1, 3))
GROUPED = {"wu00": "ga", "wu01": "gb", "wu10": "ga", "wu11": "gv", "wd0": "ga", "wd1": "gv"}
WEAVE = {"wu00": "SS", "wu01": "SS", "wu10": "SS", "wu11": "VV", "wd0": "SS", "wd1": "VV"}


def tile_list_modp_silu_resP_kernel(
    tc, tab_words, tab_scales, wu, sm, wd, rT, wgo, offs, out_0, out_1, out_2
):
    nc = tc.nc
    with ExitStack() as ctx:
        keep = ctx.enter_context(tc.tile_pool(name="keep", bufs=1))
        big = ctx.enter_context(tc.tile_pool(name="big", bufs=4))
        work = ctx.enter_context(tc.tile_pool(name="work", bufs=3))
        ps1 = ctx.enter_context(tc.psum_pool(name="ps1", bufs=4))
        ps2 = ctx.enter_context(tc.psum_pool(name="ps2", bufs=4))

        offsets = keep.tile([P, J // 16], U16, name="offsets")
        nc.sync.dma_start(offsets[:], offs)

        smt = keep.tile([P, 2, PACK], F32, name="smt")
        nc.sync.dma_start(smt[:], sm.rearrange("(b p t) -> p b t", b=2, t=PACK))
        tabs = keep.tile([P, T], U8, name="tabs", tag="tabs", align_bytes=64)
        nc.gpsimd.memset(tabs[:].bitcast(I32), 0)
        gs1 = keep.tile([P, J], U8, name="gs1", align_bytes=64)
        nc.gpsimd.memset(gs1[:].bitcast(I32), 0)
        for q in range(4):
            nc.sync.dma_start(
                tabs[32 * q : 32 * q + 8, :].bitcast(I32),
                tab_scales[:, 4 * q : 4 * q + 4, :].bitcast(I32),
            )

        def weight_block(rows, name, engines):
            raw = big.tile([P, T], F32, name="raw_" + name, tag="big", align_bytes=64)
            queue = nc.scalar if name == "wu00" else nc.sync
            queue.dma_start(
                raw[:].rearrange("p (j c) -> p j c", j=PACK), rows.rearrange("(p j) c -> p j c", j=PACK)
            )
            grouped = keep.tile([P, PACK * KP], BF16, name="grp_" + name, tag=GROUPED[name], align_bytes=64)
            dst = grouped[:].rearrange("p (t m j) -> p m j t", t=PACK, j=PACK)
            srcv = raw[:].rearrange("p (j m t) -> p m j t", j=PACK, t=PACK)
            if engines == "VV":
                nc.vector.tensor_copy(dst, srcv)
            else:
                for u in range(2):
                    copy = nc.vector.tensor_copy if engines[u] == "V" else nc.scalar.copy
                    copy(dst[:, 64 * u : 64 * (u + 1)], srcv[:, 64 * u : 64 * (u + 1)])
            tag = "tabs" if name == "wu00" else "codes_" + name
            codes = keep.tile([P, KP], U32, name="codes_" + name, tag=tag, align_bytes=64)
            scales = keep.tile([P, KP], U8, name="scales_" + name, align_bytes=64)
            nc.vector.quantize_mx(codes[:].bitcast(FP8X4), scales[:], grouped[:])
            return codes, scales

        def wu_block(b, a):
            name = "wu%d%d" % (b, a)
            return weight_block(wu[KP * a : KP * (a + 1), KP * b : KP * (b + 1)], name, WEAVE[name])

        tabw = big.tile([P, T], I32, name="tabw", tag="big", align_bytes=64)
        nc.scalar.dma_start(tabw[:], tab_words[0].rearrange("p t b -> p (t b)").bitcast(I32))
        gw = keep.tile([P, J], U32, name="gw", tag="gw", align_bytes=64)
        nc.vector.tensor_copy(gw[:], tabw[:].bitcast(U32).indirect(offsets[:]))
        parted = keep.tile([P, 2 * J], U16, name="parted", align_bytes=64)
        nc.vector.tensor_copy(
            parted[:].rearrange("p (d j) -> p d j", d=2),
            gw[:].bitcast(U16).rearrange("p (j d) -> p d j", d=2),
        )
        gs0 = keep.tile([P, J], U8, name="gs0", tag="gw", align_bytes=64)
        nc.vector.tensor_copy(gs0[:], tabs[:].indirect(offsets[:]))
        for q in range(4):
            nc.sync.dma_start(
                gs1[32 * q : 32 * q + 4, :].bitcast(I32), gs0[32 * q + 4 : 32 * q + 8, :].bitcast(I32)
            )
        gsc = [gs0, gs1]
        wuq = {(b, a): wu_block(b, a) for b in range(2) for a in range(2)}

        hq = {}
        for b in range(2):
            for half in range(2):
                hq[b, half] = (
                    keep.tile([P, KP], U32, name="hc%d%d" % (b, half), align_bytes=64),
                    keep.tile([P, KP], U8, name="hs%d%d" % (b, half), align_bytes=64),
                )

        def up(out, b, t, j0, width):
            for a in range(2):
                codes, scales = wuq[b, a]
                nc.tensor.matmul_mx(
                    out,
                    lhsT=codes[:, P * t : P * (t + 1)].bitcast(FP8X4),
                    lhsT_scale=scales[:, P * t : P * (t + 1)],
                    rhs=parted[:, a * J + j0 : a * J + j0 + width].bitcast(FP4X4),
                    rhs_scale=gsc[a][:, j0 : j0 + width],
                    start=(a == 0),
                    stop=(a == 1),
                )

        def hidden(b, g):
            j0 = g * GRP
            act = work.tile([P, PACK * GRP], F32, name="act", tag="act", align_bytes=64)
            hb = work.tile([P, PACK * GRP], BF16, name="hb", tag="hb", align_bytes=64)
            if (b, g) in ON_SCALAR:
                pairs = work.tile([P, 2, GRP, 2], BF16, name="pairs", tag="pairs", bufs=2, align_bytes=64)
                for u in range(2):
                    bank = ps1.tile([P, 2 * GRP], F32, name="a_bank", tag="a")
                    for e in range(2):
                        up(bank[:, e * GRP : (e + 1) * GRP], b, 2 * u + e, j0, GRP)
                    nc.scalar.activation(act[:, 2 * u * GRP : 2 * (u + 1) * GRP], bank[:], ACT.Silu)
                    for e in range(2):
                        t = 2 * u + e
                        nc.scalar.activation(
                            pairs[:, u, :, e], act[:, t * GRP : (t + 1) * GRP], ACT.Copy, scale=smt[:, b, t : t + 1]
                        )
                nc.vector.tensor_copy(
                    hb[:].bitcast(F32).rearrange("p (j u) -> p j u", u=2),
                    pairs[:].rearrange("p u j e -> p (u j e)").bitcast(F32).rearrange("p (u j) -> p j u", u=2),
                )
            else:
                for c in range(GRP // CH):
                    bank = ps1.tile([P, PACK * CH], F32, name="a_bank", tag="a")
                    for t in range(PACK):
                        up(bank[:, t * CH : (t + 1) * CH], b, t, j0 + c * CH, CH)
                    nc.scalar.activation(
                        act[:, c * KP : (c + 1) * KP].rearrange("p (j t) -> p j t", t=PACK),
                        bank[:].rearrange("p (t j) -> p j t", t=PACK),
                        ACT.Silu,
                    )
                nc.vector.tensor_tensor(
                    hb[:].rearrange("p (j t) -> p j t", t=PACK),
                    act[:].rearrange("p (j t) -> p j t", t=PACK),
                    smt[:, b : b + 1, :].to_broadcast([P, GRP, PACK]),
                    ALU.mult,
                )
            codes, scales = hq[b, j0 // KP]
            o = j0 % KP
            nc.vector.quantize_mx(codes[:, o : o + GRP].bitcast(FP8X4), scales[:, o : o + GRP], hb[:])

        for b in range(2):
            hidden(b, 0)
        wdq = [weight_block(wd[KP * b : KP * (b + 1), :], "wd%d" % b, WEAVE["wd%d" % b]) for b in range(2)]

        pages = []
        for i in range(PACK):
            page = keep.tile([P, T], F32, name="page%d" % i, tag="page%d" % i, align_bytes=64)
            nc.vector.memset(page[:], 0.0)
            pages.append(page)

        wg = big.tile([P, J], F32, name="wg", tag="big", align_bytes=64)
        nc.sync.dma_start(wg[:, :GRP], wgo[:, :GRP])
        rts = []
        for i in range(PACK):
            rt = big.tile([P, T], F32, name="rt%d" % i, tag="big", align_bytes=64)
            nc.sync.dma_start(rt[:], rT.rearrange("(p i) t -> p i t", i=PACK)[:, i, :])
            rts.append(rt)
            if i == 0:
                nc.sync.dma_start(wg[:, GRP:], wgo[:, GRP:])

        def place(i, j0, width, last=False):
            half, o = j0 // KP, j0 % KP
            bank = ps2.tile([P, KP], F32, name="y_bank", tag="y")
            for b in range(2):
                nc.tensor.matmul_mx(
                    bank[:, :width],
                    lhsT=wdq[b][0][:, P * i : P * (i + 1)].bitcast(FP8X4),
                    lhsT_scale=wdq[b][1][:, P * i : P * (i + 1)],
                    rhs=hq[b, half][0][:, o : o + width].bitcast(FP8X4),
                    rhs_scale=hq[b, half][1][:, o : o + width],
                    start=(b == 0),
                    stop=(b == 1),
                )
            if last:
                y = keep.tile([P, KP], F32, name="y_last", tag="page2", align_bytes=64)
            else:
                y = work.tile([P, KP], F32, name="y", tag="y", bufs=4, align_bytes=64)
            nc.scalar.copy(y[:, :width], bank[:, :width])
            sl = offsets[:, j0 // 16 : (j0 + width) // 16]
            z = work.tile([P, KP], F32, name="z", tag="z", align_bytes=64)
            nc.vector.tensor_tensor(z[:, :width], rts[i][:].indirect(sl), y[:, :width], ALU.add)
            nc.vector.tensor_tensor(pages[i][:].indirect(sl), z[:, :width], wg[:, j0 : j0 + width], ALU.mult)

        woven = [keep.tile([P, OC, PACK], BF16, name="woven%d" % c, align_bytes=64) for c in range(T // OC)]
        ocodes = [keep.tile([P, OC], U32, name="ocodes%d" % c, align_bytes=64) for c in range(T // OC)]
        oscales = keep.tile([P, T], U8, name="oscales", align_bytes=64)
        out_rows = out_0.rearrange("(p i) t -> p i t", i=PACK)
        out_words = out_1[0].rearrange("p t b -> p (t b)").bitcast(I32)

        def finish(i):
            nc.sync.dma_start(out_rows[:, i, :], pages[i][:])
            for c in (2, 3, 0, 1):
                if i == PACK - 1 and c >= 2:
                    nc.vector.tensor_copy(woven[c][:, :, i], pages[i][:, c * OC : (c + 1) * OC])
                else:
                    nc.scalar.copy(woven[c][:, :, i], pages[i][:, c * OC : (c + 1) * OC])
                if i == PACK - 1:
                    nc.vector.quantize_mx(
                        ocodes[c][:].bitcast(FP8X4),
                        oscales[:, c * OC : (c + 1) * OC],
                        woven[c][:].rearrange("p j t -> p (j t)"),
                    )
                    nc.sync.dma_start(out_words[:, c * OC : (c + 1) * OC], ocodes[c][:].bitcast(I32))

        for g in range(J // GRP):
            place(0, g * GRP, GRP)
            if g + 1 < J // GRP:
                for b in range(2):
                    hidden(b, g + 1)
        for i in range(1, PACK - 1):
            for half in range(2):
                place(i, half * KP, KP)
            finish(i - 1)
        place(3, 0, KP)
        place(3, KP, GRP)
        finish(2)
        place(3, KP + GRP, GRP, last=True)
        finish(3)
        for q in range(4):
            nc.scalar.dma_start(
                out_2[0, 4 * q : 4 * q + 4, :].bitcast(I32), oscales[32 * q : 32 * q + 4, :].bitcast(I32)
            )
